import numpy as np
import ml_dtypes


def mxq(x, axis, fmt="e4m3"):
    dtype, down = {"e4m3": (ml_dtypes.float8_e4m3fn, 7), "e5m2": (ml_dtypes.float8_e5m2, 14)}[fmt]
    v = np.moveaxis(np.asarray(x, np.float32).astype(ml_dtypes.bfloat16).astype(np.float64), axis, -1)
    blocks = v.reshape(v.shape[:-1] + (-1, 32))
    amax = np.abs(blocks).max(-1, keepdims=True)
    byte = np.maximum(np.where(amax > 0, np.frexp(amax)[1] - 1 + 127, 0) - down, 1)
    scale = np.exp2(byte - 127.0)
    codes = (blocks / scale).astype(np.float32).astype(dtype).astype(np.float64)
    return np.moveaxis((codes * scale).reshape(v.shape), -1, axis)


WIDE = False


def mx_kscale(k):
    if not WIDE:
        return np.ones(k)
    levels = np.array([30, -30])
    if k % 512:
        return np.exp2(np.random.permutation(np.resize(levels, k // 32))).repeat(32)
    a = np.empty((k // 512, 16))
    for p in range(k // 512):
        a[p, :8] = np.random.permutation(np.resize(levels, 8))
        for g in range(8):
            far = levels[np.abs(levels - a[p, g]) >= 10]
            a[p, g + 8] = far[np.random.randint(len(far))]
    return np.exp2(a.ravel()).repeat(32)


def f64(x):
    return np.asarray(x).astype(np.float64)


def striped(idx):
    return np.tile(np.asarray(idx).reshape(-1, 16).T, (8, 1)).astype(np.uint16)


def unstriped(offs):
    return offs[:16].T.reshape(-1).astype(np.int64)


E2M1 = np.array([0.0, 0.5, 1.0, 1.5, 2.0, 3.0, 4.0, 6.0, -0.0, -0.5, -1.0, -1.5, -2.0, -3.0, -4.0, -6.0])


def pack_weight(w, fmt):
    k, n = w.shape
    w = f64(np.asarray(w, np.float32).astype(ml_dtypes.bfloat16)).reshape(k // 32, 32, n)
    amax = np.abs(w).max(1)
    if fmt == "e4m3":
        byte = np.frexp(amax)[1] - 1 + 127 - 7
    else:
        mant, ex = np.frexp(amax / 6.0)
        byte = np.where(mant > 0.5, ex, ex - 1) + 127
    byte = np.clip(np.where(amax > 0, byte, 1), 1, 254)
    scaled = (w * np.exp2(127.0 - byte)[:, None, :]).reshape(k, n).astype(np.float32)
    by_word = np.ascontiguousarray(scaled.reshape(k // 512, 128, 4, n).transpose(0, 1, 3, 2))
    if fmt == "e4m3":
        words = by_word.astype(ml_dtypes.float8_e4m3fn).view(np.uint8)
    else:
        c = by_word.astype(ml_dtypes.float4_e2m1fn).view(np.uint8) & 0xF
        words = (c[..., 0::2] | (c[..., 1::2] << 4)).reshape(k // 512, 128, 2 * n)
    return np.ascontiguousarray(words), np.ascontiguousarray(byte.astype(np.uint8).reshape(k // 512, 16, n))


def unpack_weight(words, scales, fmt):
    g, _, n = scales.shape
    words = np.ascontiguousarray(words).reshape(g, 128, n, -1)
    if fmt == "e4m3":
        vals = words.view(ml_dtypes.float8_e4m3fn).astype(np.float64)
    else:
        nib = np.empty((g, 128, n, 4), np.uint8)
        nib[..., 0::2] = words & 0xF
        nib[..., 1::2] = words >> 4
        vals = E2M1[nib]
    vals = vals * np.repeat(np.exp2(scales.astype(np.float64) - 127.0), 8, axis=1)[..., None]
    return vals.transpose(0, 1, 3, 2).reshape(g * 512, n)


def sigmoid(v):
    return 1.0 / (1.0 + np.exp(-v))


K, F, T, Z, J, R, O, N, E = 512, 512, 1024, 1024, 256, 512, 128, 256, 1024


def setup_inputs():
    n = np.random.standard_normal
    idx = np.random.permutation(T)[:J]
    idx2 = np.random.permutation(Z)[:J]
    idx3 = np.random.permutation(J)[:O]
    idx4 = np.random.permutation(J)[:O]
    idx5 = np.random.permutation(E)[:O]
    fk = mx_kscale(K)
    ff = mx_kscale(F)
    fr = mx_kscale(R)
    xtp = pack_weight(n((K, T)) / fk[:, None], "e2m1")
    wp = pack_weight(n((K, R)) * 1 / np.sqrt(K) * fk[:, None], "e4m3")
    xop = pack_weight(n((F, Z)) / ff[:, None], "e4m3")
    w2p = pack_weight(n((F, R)) * 1 / np.sqrt(F) * ff[:, None] * fr, "e2m1")
    wbp = pack_weight(n((R, N)) * 1 / np.sqrt(R) / fr[:, None], "e2m1")
    return {
        "xt_words": xtp[0],
        "xt_scales": xtp[1],
        "w_words": wp[0],
        "w_scales": wp[1],
        "xo_words": xop[0],
        "xo_scales": xop[1],
        "w2_words": w2p[0],
        "w2_scales": w2p[1],
        "sg": (np.random.uniform(0.6, 1.6, (R, 1))).astype(np.float32),
        "wb_words": wbp[0],
        "wb_scales": wbp[1],
        "offs": striped(idx),
        "offs2": striped(idx2),
        "offs3": striped(idx3),
        "offs4": striped(idx4),
        "offs5": striped(idx5),
    }


def reference(xt_words, xt_scales, w_words, w_scales, xo_words, xo_scales, w2_words, w2_scales, sg, wb_words, wb_scales, offs, offs2, offs3, offs4, offs5):
    idx = unstriped(offs)
    idx2 = unstriped(offs2)
    idx3 = unstriped(offs3)
    idx4 = unstriped(offs4)
    idx5 = unstriped(offs5)
    xtu = unpack_weight(xt_words, xt_scales, "e2m1")
    wu = unpack_weight(w_words, w_scales, "e4m3")
    xou = unpack_weight(xo_words, xo_scales, "e4m3")
    w2u = unpack_weight(w2_words, w2_scales, "e2m1")
    wbu = unpack_weight(wb_words, wb_scales, "e2m1")
    xtidxg = xtu[:, idx]
    a = wu.T @ xtidxg
    xoidx2g = xou[:, idx2]
    b = w2u.T @ xoidx2g
    hid = np.maximum(b[:, idx3], b[:, idx4]) * sigmoid(a[:, idx4] * f64(sg))
    hidq = mxq(hid, 0, "e5m2")
    p = wbu.T @ hidq
    y = np.zeros((N, E))
    y[:, idx5] = p
    return y

@@ -1,0 +1,150 @@
+from contextlib import ExitStack
+
+import concourse.mybir as mybir
+
+F32 = mybir.dt.float32
+BF16 = mybir.dt.bfloat16
+I32 = mybir.dt.int32
+U32 = mybir.dt.uint32
+U16 = mybir.dt.uint16
+U8 = mybir.dt.uint8
+E4M3 = mybir.dt.float8_e4m3fn_x4
+E5M2 = mybir.dt.float8_e5m2_x4
+E2M1 = mybir.dt.float4_e2m1fn_x4
+ACT = mybir.ActivationFunctionType
+ALU = mybir.AluOpType
+
+P = 128
+PACK = 4
+T, Z, J, R, O, N, E = 1024, 1024, 256, 512, 128, 256, 1024
+FLOPS = 2 * 512 * R * J * 2 + 2 * R * N * O
+
+
+def tile_list_twotab_agree_one_scattered_kernel(tc, xt_words, xt_scales, w_words, w_scales, xo_words, xo_scales,
+        w2_words, w2_scales, sg, wb_words, wb_scales, offs, offs2, offs3, offs4, offs5, out):
+    nc = tc.nc
+    with ExitStack() as ctx:
+        keep = ctx.enter_context(tc.tile_pool(name="keep", bufs=1))
+        psum = ctx.enter_context(tc.psum_pool(name="psum", bufs=1))
+
+        def tile(name, shape, dtype):
+            return keep.tile(shape, dtype, name=name, align_bytes=64)
+
+        def load_list(name, src):
+            dst = keep.tile(list(src.shape), U16, name=name)
+            nc.sync.dma_start(dst[:], src)
+            return dst
+
+        def load_words(name, src, columns, dtype, engine):
+            dst = tile(name, [P, columns], dtype)
+            engine.dma_start(dst[:].bitcast(I32), src.bitcast(I32))
+            return dst
+
+        def zeroed_plane(name, columns):
+            plane = tile(name, [P, columns], U8)
+            nc.vector.memset(plane[:].bitcast(I32), 0)
+            return plane
+
+        def load_scale_rows(plane, src, engines):
+            for q, engine in enumerate(engines):
+                engine.dma_start(plane[:].bitcast(I32)[32 * q : 32 * q + 4, :], src[0].bitcast(I32)[4 * q : 4 * q + 4, :])
+
+        def deal(name, src, dtype, run, view=None):
+            dst = tile(name, [P, PACK, P], dtype)
+            src_ap, dst_ap = (src[:], dst[:]) if view is None else (src[:].bitcast(view), dst[:].bitcast(view))
+            nc.vector.tensor_copy(
+                out=dst_ap.rearrange("p t (c i) -> p c t i", i=run),
+                in_=src_ap.rearrange("p (c i t) -> p c t i", i=run, t=PACK))
+            return dst
+
+        def gather(name, window, offsets, columns, dtype):
+            dst = tile(name, [P, columns], dtype)
+            nc.vector.tensor_copy(dst[:], window[:].indirect(offsets[:]))
+            return dst
+
+        xt_s = zeroed_plane("xt_s", T)
+        w_s = zeroed_plane("w_s", R)
+        xo_s = zeroed_plane("xo_s", Z)
+        w2_s = zeroed_plane("w2_s", R)
+        wb_s = zeroed_plane("wb_s", N)
+        pages = [tile(f"page{h}", [P, E], F32) for h in range(2)]
+        for page in pages:
+            nc.vector.memset(page[:], 0.0)
+
+        both_queues = [nc.sync, nc.scalar] * 2
+        idx = load_list("idx", offs)
+        xt_w = load_words("xt_w", xt_words[0], T, U16, nc.sync)
+        w_w = load_words("w_w", w_words[0].rearrange("p n t -> p (n t)"), R, U32, nc.sync)
+        idx2 = load_list("idx2", offs2)
+        load_scale_rows(xt_s, xt_scales, both_queues)
+        load_scale_rows(w_s, w_scales, both_queues)
+        xo_w = load_words("xo_w", xo_words[0].rearrange("p n t -> p (n t)"), Z, U32, nc.sync)
+        idx4 = load_list("idx4", offs4)
+        w2_w = load_words("w2_w", w2_words[0], R, U16, nc.sync)
+        load_scale_rows(xo_s, xo_scales, both_queues)
+        load_scale_rows(w2_s, w2_scales, [nc.sync] * 4)
+        idx3 = load_list("idx3", offs3)
+        idx5 = load_list("idx5", offs5)
+        slope = tile("slope", [P, PACK], F32)
+        nc.gpsimd.dma_start(slope[:], sg.rearrange("(p t) o -> p (t o)", t=PACK))
+        wb_w = load_words("wb_w", wb_words[0], N, U16, nc.gpsimd)
+        load_scale_rows(wb_s, wb_scales, [nc.gpsimd] * 4)
+
+        xt_gw = gather("xt_gw", xt_w, idx, J, U16)
+        xt_gs = gather("xt_gs", xt_s, idx, J, U8)
+        w_dw = deal("w_dw", w_w, U32, 4, I32)
+        w_ds = deal("w_ds", w_s, U8, 16)
+
+        gate = tile("gate", [P, PACK, O], F32)
+        for t in range(PACK):
+            bank = psum.tile([P, J], F32, name=f"bank{t}")
+            nc.tensor.matmul_mx(out=bank[:], lhsT=w_dw[:, t, :].bitcast(E4M3), lhsT_scale=w_ds[:, t, :],
+                                rhs=xt_gw[:].bitcast(E2M1), rhs_scale=xt_gs[:], start=True, stop=True)
+            a_t = keep.tile([P, J], F32, name=f"a{t % 2}", align_bytes=64)
+            if t < 2:
+                nc.vector.tensor_copy(a_t[:], bank[:])
+            else:
+                nc.scalar.copy(a_t[:], bank[:])
+            nc.scalar.activation(out=gate[:, t, :], in_=a_t[:].indirect(idx4[:]), func=ACT.Sigmoid, scale=slope[:, t : t + 1])
+
+        xo_gw = gather("xo_gw", xo_w, idx2, J, U32)
+        w2_dw = deal("w2_dw", w2_w, U16, 8)
+        xo_gs = gather("xo_gs", xo_s, idx2, J, U8)
+        w2_ds = deal("w2_ds", w2_s, U8, 16)
+
+        b3 = tile("b3", [P, PACK, O], F32)
+        b4 = tile("b4", [P, PACK, O], F32)
+        top = tile("top", [P, PACK, O], F32)
+        for t in range(PACK):
+            bank = psum.tile([P, J], F32, name=f"bank{PACK + t}")
+            nc.tensor.matmul_mx(out=bank[:], lhsT=w2_dw[:, t, :].bitcast(E2M1), lhsT_scale=w2_ds[:, t, :],
+                                rhs=xo_gw[:].bitcast(E4M3), rhs_scale=xo_gs[:], start=True, stop=True)
+            b_t = tile(f"b_rows{t}", [P, J], F32)
+            nc.scalar.copy(b_t[:], bank[:])
+            nc.scalar.activation(out=b3[:, t, :], in_=b_t[:].indirect(idx3[:]), func=ACT.Copy)
+            nc.vector.tensor_copy(b4[:, t, :], b_t[:].indirect(idx4[:]))
+            nc.vector.tensor_tensor(top[:, t, :], b3[:, t, :], b4[:, t, :], ALU.max)
+
+        hid = tile("hid", [P, O, PACK], BF16)
+        nc.vector.tensor_tensor(
+            hid[:].rearrange("p (c i) t -> p c t i", i=4),
+            top[:].rearrange("p t (c i) -> p c t i", i=4),
+            gate[:].rearrange("p t (c i) -> p c t i", i=4), ALU.mult)
+        hid_w = tile("hid_w", [P, O], U32)
+        hid_s = tile("hid_s", [P, O], U8)
+        nc.vector.quantize_mx(out=hid_w[:].bitcast(E5M2), scales=hid_s[:], in_=hid[:].rearrange("p o t -> p (o t)"))
+
+        for h in range(2):
+            rows = slice(h * P, (h + 1) * P)
+            bank = psum.tile([P, O], F32, name=f"bank{h}")
+            nc.tensor.matmul_mx(out=bank[:], lhsT=wb_w[:, rows].bitcast(E2M1), lhsT_scale=wb_s[:, rows],
+                                rhs=hid_w[:].bitcast(E5M2), rhs_scale=hid_s[:], start=True, stop=True)
+            p_h = tile(f"p{h}", [P, O], F32)
+            if h == 0:
+                nc.vector.tensor_copy(p_h[:], bank[:])
+                nc.vector.tensor_copy(pages[h][:].indirect(idx5[:]), p_h[:])
+                nc.sync.dma_start(out[rows, :], pages[h][:])
+            else:
+                nc.scalar.copy(p_h[:], bank[:])
+                nc.scalar.activation(out=pages[h][:].indirect(idx5[:]), in_=p_h[:], func=ACT.Copy)
+                nc.scalar.dma_start(out[rows, :], pages[h][:])

@@ -45,85 +45,115 @@ def tile_list_twotab_agree_one_scattered_kernel(tc, xt_words, xt_scales, w_words
             nc.vector.memset(plane[:].bitcast(I32), 0)
             return plane
 
-        def load_scale_rows(plane, src, engines):
-            for q, engine in enumerate(engines):
-                engine.dma_start(plane[:].bitcast(I32)[32 * q : 32 * q + 4, :], src[0].bitcast(I32)[4 * q : 4 * q + 4, :])
+        def load_scale_rows(dst, src, engine):
+            engine.dma_start(dst.bitcast(I32)[0:16, :], src[0].bitcast(I32))
 
-        def deal(name, src, dtype, run, view=None):
-            dst = tile(name, [P, PACK, P], dtype)
-            src_ap, dst_ap = (src[:], dst[:]) if view is None else (src[:].bitcast(view), dst[:].bitcast(view))
+        def spread_scale_rows(planes):
+            words = planes[:].bitcast(I32)
+            for q in range(1, 4):
+                nc.sync.dma_start(words[32 * q : 32 * q + 4, :], words[4 * q : 4 * q + 4, :])
+
+        def deal(dst, src, run):
             nc.vector.tensor_copy(
-                out=dst_ap.rearrange("p t (c i) -> p c t i", i=run),
-                in_=src_ap.rearrange("p (c i t) -> p c t i", i=run, t=PACK))
-            return dst
+                out=dst.rearrange("p (t c i) -> p c t i", t=PACK, i=run),
+                in_=src.rearrange("p (c i t) -> p c t i", i=run, t=PACK))
 
         def gather(name, window, offsets, columns, dtype):
             dst = tile(name, [P, columns], dtype)
             nc.vector.tensor_copy(dst[:], window[:].indirect(offsets[:]))
             return dst
 
+        warm = tile("warm", [P, 2], F32)
+        nc.gpsimd.memset(warm[:, 0:1], 0.0)
+        nc.scalar.activation(out=warm[:, 1:2], in_=warm[:, 0:1], func=ACT.Sigmoid)
+
         xt_s = zeroed_plane("xt_s", T)
         w_s = zeroed_plane("w_s", R)
         xo_s = zeroed_plane("xo_s", Z)
         w2_s = zeroed_plane("w2_s", R)
-        wb_s = zeroed_plane("wb_s", N)
+        planes_a = tile("planes_a", [P, J + R], U8)
+        planes_b = tile("planes_b", [P, J + R + N], U8)
+        wb_s = planes_b[:, J + R :]
+        nc.vector.memset(wb_s.bitcast(I32), 0)
         pages = [tile(f"page{h}", [P, E], F32) for h in range(2)]
         for page in pages:
             nc.vector.memset(page[:], 0.0)
 
-        both_queues = [nc.sync, nc.scalar] * 2
         idx = load_list("idx", offs)
+        idx2 = load_list("idx2", offs2)
+        load_scale_rows(xt_s[:], xt_scales, nc.sync)
+        load_scale_rows(w_s[:], w_scales, nc.sync)
+        load_scale_rows(xo_s[:], xo_scales, nc.sync)
+        load_scale_rows(w2_s[:], w2_scales, nc.sync)
         xt_w = load_words("xt_w", xt_words[0], T, U16, nc.sync)
         w_w = load_words("w_w", w_words[0].rearrange("p n t -> p (n t)"), R, U32, nc.sync)
-        idx2 = load_list("idx2", offs2)
-        load_scale_rows(xt_s, xt_scales, both_queues)
-        load_scale_rows(w_s, w_scales, both_queues)
         xo_w = load_words("xo_w", xo_words[0].rearrange("p n t -> p (n t)"), Z, U32, nc.sync)
         idx4 = load_list("idx4", offs4)
-        w2_w = load_words("w2_w", w2_words[0], R, U16, nc.sync)
-        load_scale_rows(xo_s, xo_scales, both_queues)
-        load_scale_rows(w2_s, w2_scales, [nc.sync] * 4)
         idx3 = load_list("idx3", offs3)
         idx5 = load_list("idx5", offs5)
+        w2_w = load_words("w2_w", w2_words[0], R, U16, nc.sync)
+        load_scale_rows(wb_s, wb_scales, nc.gpsimd)
         slope = tile("slope", [P, PACK], F32)
         nc.gpsimd.dma_start(slope[:], sg.rearrange("(p t) o -> p (t o)", t=PACK))
         wb_w = load_words("wb_w", wb_words[0], N, U16, nc.gpsimd)
-        load_scale_rows(wb_s, wb_scales, [nc.gpsimd] * 4)
+
+        xt_gs = gather("xt_gs", xt_s, idx, J, U8)
+        deal(planes_a[:, J:], w_s[:], 16)
+        nc.vector.tensor_copy(planes_a[:, :J].bitcast(I32), xt_gs[:].bitcast(I32))
+        spread_scale_rows(planes_a)
+        xo_gs = gather("xo_gs", xo_s, idx2, J, U8)
+        deal(planes_b[:, J : J + R], w2_s[:], 16)
+        nc.vector.tensor_copy(planes_b[:, :J].bitcast(I32), xo_gs[:].bitcast(I32))
+        spread_scale_rows(planes_b)
 
         xt_gw = gather("xt_gw", xt_w, idx, J, U16)
-        xt_gs = gather("xt_gs", xt_s, idx, J, U8)
-        w_dw = deal("w_dw", w_w, U32, 4, I32)
-        w_ds = deal("w_ds", w_s, U8, 16)
+        w_dw = tile("w_dw", [P, R], U32)
+        deal(w_dw[:].bitcast(I32), w_w[:].bitcast(I32), 4)
 
         gate = tile("gate", [P, PACK, O], F32)
         for t in range(PACK):
             bank = psum.tile([P, J], F32, name=f"bank{t}")
-            nc.tensor.matmul_mx(out=bank[:], lhsT=w_dw[:, t, :].bitcast(E4M3), lhsT_scale=w_ds[:, t, :],
-                                rhs=xt_gw[:].bitcast(E2M1), rhs_scale=xt_gs[:], start=True, stop=True)
-            a_t = keep.tile([P, J], F32, name=f"a{t % 2}", align_bytes=64)
+            nc.tensor.matmul_mx(out=bank[:], lhsT=w_dw[:, t * P : (t + 1) * P].bitcast(E4M3),
+                                lhsT_scale=planes_a[:, J + t * P : J + (t + 1) * P],
+                                rhs=xt_gw[:].bitcast(E2M1), rhs_scale=planes_a[:, :J], start=True, stop=True)
+            a_t = tile(f"a_rows{t}", [P, J], F32)
             if t < 2:
-                nc.vector.tensor_copy(a_t[:], bank[:])
-            else:
                 nc.scalar.copy(a_t[:], bank[:])
+            else:
+                nc.vector.tensor_copy(a_t[:], bank[:])
             nc.scalar.activation(out=gate[:, t, :], in_=a_t[:].indirect(idx4[:]), func=ACT.Sigmoid, scale=slope[:, t : t + 1])
 
         xo_gw = gather("xo_gw", xo_w, idx2, J, U32)
-        w2_dw = deal("w2_dw", w2_w, U16, 8)
-        xo_gs = gather("xo_gs", xo_s, idx2, J, U8)
-        w2_ds = deal("w2_ds", w2_s, U8, 16)
+        w2_dw = tile("w2_dw", [P, R], U16)
+        deal(w2_dw[:], w2_w[:], 8)
 
         b3 = tile("b3", [P, PACK, O], F32)
         b4 = tile("b4", [P, PACK, O], F32)
         top = tile("top", [P, PACK, O], F32)
-        for t in range(PACK):
-            bank = psum.tile([P, J], F32, name=f"bank{PACK + t}")
-            nc.tensor.matmul_mx(out=bank[:], lhsT=w2_dw[:, t, :].bitcast(E2M1), lhsT_scale=w2_ds[:, t, :],
-                                rhs=xo_gw[:].bitcast(E4M3), rhs_scale=xo_gs[:], start=True, stop=True)
-            b_t = tile(f"b_rows{t}", [P, J], F32)
-            nc.scalar.copy(b_t[:], bank[:])
-            nc.scalar.activation(out=b3[:, t, :], in_=b_t[:].indirect(idx3[:]), func=ACT.Copy)
-            nc.vector.tensor_copy(b4[:, t, :], b_t[:].indirect(idx4[:]))
-            nc.vector.tensor_tensor(top[:, t, :], b3[:, t, :], b4[:, t, :], ALU.max)
+        for half in range(2):
+            bank = psum.tile([P, 2 * J], F32, name=f"bank{PACK + half}")
+            for u in range(2):
+                t = 2 * half + u
+                nc.tensor.matmul_mx(out=bank[:, u * J : (u + 1) * J], lhsT=w2_dw[:, t * P : (t + 1) * P].bitcast(E2M1),
+                                    lhsT_scale=planes_b[:, J + t * P : J + (t + 1) * P],
+                                    rhs=xo_gw[:].bitcast(E4M3), rhs_scale=planes_b[:, :J], start=True, stop=True)
+            b_pair = tile(f"b_pair{half}", [P, 2 * J], F32)
+            if half == 0:
+                nc.vector.tensor_copy(b_pair[:], bank[:])
+            else:
+                nc.scalar.copy(b_pair[:], bank[:])
+            for u in range(2):
+                t = 2 * half + u
+                b_t = b_pair[:, u * J : (u + 1) * J]
+                if t < 1:
+                    nc.vector.tensor_copy(b3[:, t, :], b_t.indirect(idx3[:]))
+                else:
+                    nc.scalar.activation(out=b3[:, t, :], in_=b_t.indirect(idx3[:]), func=ACT.Copy)
+                if t < 3:
+                    nc.vector.tensor_copy(b4[:, t, :], b_t.indirect(idx4[:]))
+                else:
+                    nc.scalar.activation(out=b4[:, t, :], in_=b_t.indirect(idx4[:]), func=ACT.Copy)
+                nc.vector.tensor_tensor(top[:, t, :], b3[:, t, :], b4[:, t, :], ALU.max)
 
         hid = tile("hid", [P, O, PACK], BF16)
         nc.vector.tensor_tensor(
@@ -137,7 +167,7 @@ def tile_list_twotab_agree_one_scattered_kernel(tc, xt_words, xt_scales, w_words
         for h in range(2):
             rows = slice(h * P, (h + 1) * P)
             bank = psum.tile([P, O], F32, name=f"bank{h}")
-            nc.tensor.matmul_mx(out=bank[:], lhsT=wb_w[:, rows].bitcast(E2M1), lhsT_scale=wb_s[:, rows],
+            nc.tensor.matmul_mx(out=bank[:], lhsT=wb_w[:, rows].bitcast(E2M1), lhsT_scale=planes_b[:, J + R + h * P : J + R + (h + 1) * P],
                                 rhs=hid_w[:].bitcast(E5M2), rhs_scale=hid_s[:], start=True, stop=True)
             p_h = tile(f"p{h}", [P, O], F32)
             if h == 0:

@@ -45,13 +45,13 @@ def tile_list_twotab_agree_one_scattered_kernel(tc, xt_words, xt_scales, w_words
             nc.vector.memset(plane[:].bitcast(I32), 0)
             return plane
 
-        def load_scale_rows(dst, src, engine):
-            engine.dma_start(dst.bitcast(I32)[0:16, :], src[0].bitcast(I32))
+        def load_scale_rows(dst, first, src, engine):
+            engine.dma_start(dst.bitcast(I32)[first : first + 16, :], src[0].bitcast(I32))
 
-        def spread_scale_rows(planes):
-            words = planes[:].bitcast(I32)
-            for q in range(1, 4):
-                nc.sync.dma_start(words[32 * q : 32 * q + 4, :], words[4 * q : 4 * q + 4, :])
+        def spread_scale_rows(dst, src, first, quadrants):
+            for q in quadrants:
+                nc.sync.dma_start(dst.bitcast(I32)[32 * q : 32 * q + 4, :],
+                                  src.bitcast(I32)[first + 4 * q : first + 4 * q + 4, :])
 
         def deal(dst, src, run):
             nc.vector.tensor_copy(
@@ -67,93 +67,82 @@ def tile_list_twotab_agree_one_scattered_kernel(tc, xt_words, xt_scales, w_words
         nc.gpsimd.memset(warm[:, 0:1], 0.0)
         nc.scalar.activation(out=warm[:, 1:2], in_=warm[:, 0:1], func=ACT.Sigmoid)
 
-        xt_s = zeroed_plane("xt_s", T)
-        w_s = zeroed_plane("w_s", R)
         xo_s = zeroed_plane("xo_s", Z)
-        w2_s = zeroed_plane("w2_s", R)
-        planes_a = tile("planes_a", [P, J + R], U8)
-        planes_b = tile("planes_b", [P, J + R + N], U8)
-        wb_s = planes_b[:, J + R :]
-        nc.vector.memset(wb_s.bitcast(I32), 0)
+        w_s = zeroed_plane("w_s", R)
+        xt_s = zeroed_plane("xt_s", T)
+        stage = tile("stage", [P, J + R + J + N], U8)
+        planes_a = zeroed_plane("planes_a", R + J + N)
         pages = [tile(f"page{h}", [P, E], F32) for h in range(2)]
         for page in pages:
             nc.vector.memset(page[:], 0.0)
 
-        idx = load_list("idx", offs)
         idx2 = load_list("idx2", offs2)
-        load_scale_rows(xt_s[:], xt_scales, nc.sync)
-        load_scale_rows(w_s[:], w_scales, nc.sync)
-        load_scale_rows(xo_s[:], xo_scales, nc.sync)
-        load_scale_rows(w2_s[:], w2_scales, nc.sync)
-        xt_w = load_words("xt_w", xt_words[0], T, U16, nc.sync)
-        w_w = load_words("w_w", w_words[0].rearrange("p n t -> p (n t)"), R, U32, nc.sync)
+        idx = load_list("idx", offs)
+        load_scale_rows(xo_s[:], 0, xo_scales, nc.sync)
+        load_scale_rows(w_s[:], 0, w2_scales, nc.sync)
+        load_scale_rows(w_s[:], 16, w_scales, nc.sync)
+        load_scale_rows(xt_s[:], 16, xt_scales, nc.sync)
         xo_w = load_words("xo_w", xo_words[0].rearrange("p n t -> p (n t)"), Z, U32, nc.sync)
+        w2_w = load_words("w2_w", w2_words[0], R, U16, nc.sync)
+        xt_w = load_words("xt_w", xt_words[0], T, U16, nc.sync)
         idx4 = load_list("idx4", offs4)
         idx3 = load_list("idx3", offs3)
         idx5 = load_list("idx5", offs5)
-        w2_w = load_words("w2_w", w2_words[0], R, U16, nc.sync)
-        load_scale_rows(wb_s, wb_scales, nc.gpsimd)
+        w_w = load_words("w_w", w_words[0].rearrange("p n t -> p (n t)"), R, U32, nc.sync)
+        load_scale_rows(stage[:, J + R + J :], 16, wb_scales, nc.gpsimd)
         slope = tile("slope", [P, PACK], F32)
         nc.gpsimd.dma_start(slope[:], sg.rearrange("(p t) o -> p (t o)", t=PACK))
         wb_w = load_words("wb_w", wb_words[0], N, U16, nc.gpsimd)
 
-        xt_gs = gather("xt_gs", xt_s, idx, J, U8)
-        deal(planes_a[:, J:], w_s[:], 16)
-        nc.vector.tensor_copy(planes_a[:, :J].bitcast(I32), xt_gs[:].bitcast(I32))
-        spread_scale_rows(planes_a)
         xo_gs = gather("xo_gs", xo_s, idx2, J, U8)
-        deal(planes_b[:, J : J + R], w2_s[:], 16)
-        nc.vector.tensor_copy(planes_b[:, :J].bitcast(I32), xo_gs[:].bitcast(I32))
-        spread_scale_rows(planes_b)
-
+        deal(stage[:, J : J + R], w_s[:], 16)
+        nc.vector.tensor_copy(stage[:, :J].bitcast(I32), xo_gs[:].bitcast(I32))
+        spread_scale_rows(stage[:, : J + R], stage[:, : J + R], 0, range(1, 4))
+        xt_gs = gather("xt_gs", xt_s, idx, J, U8)
+        nc.vector.tensor_copy(stage[:, J + R : J + R + J].bitcast(I32), xt_gs[:].bitcast(I32))
+        spread_scale_rows(planes_a[:], stage[:, J:], 16, range(4))
+        xo_gw = gather("xo_gw", xo_w, idx2, J, U32)
+        w2_dw = tile("w2_dw", [P, R], U16)
+        deal(w2_dw[:], w2_w[:], 8)
         xt_gw = gather("xt_gw", xt_w, idx, J, U16)
         w_dw = tile("w_dw", [P, R], U32)
         deal(w_dw[:].bitcast(I32), w_w[:].bitcast(I32), 4)
+
+        def empty(dst, bank, on_vector):
+            if on_vector:
+                nc.vector.tensor_copy(dst, bank)
+            else:
+                nc.scalar.copy(dst, bank)
+
+        def pick(dst, window, offsets, on_vector):
+            if on_vector:
+                nc.vector.tensor_copy(dst, window[:].indirect(offsets[:]))
+            else:
+                nc.scalar.activation(out=dst, in_=window[:].indirect(offsets[:]), func=ACT.Copy)
+
+        b3 = tile("b3", [P, PACK, O], F32)
+        b4 = tile("b4", [P, PACK, O], F32)
+        top = tile("top", [P, PACK, O], F32)
+        for t in range(PACK):
+            bank = psum.tile([P, J], F32, name=f"bank{PACK + t}")
+            nc.tensor.matmul_mx(out=bank[:], lhsT=w2_dw[:, t * P : (t + 1) * P].bitcast(E2M1),
+                                lhsT_scale=stage[:, J + t * P : J + (t + 1) * P],
+                                rhs=xo_gw[:].bitcast(E4M3), rhs_scale=stage[:, :J], start=True, stop=True)
+            b_t = tile(f"b_rows{t}", [P, J], F32)
+            empty(b_t[:], bank[:], t in ())
+            pick(b4[:, t, :], b_t, idx4, t in (0, 1, 2, 3,))
+            pick(b3[:, t, :], b_t, idx3, t in (0, 1, 2, 3,))
+        nc.vector.tensor_tensor(top[:], b3[:], b4[:], ALU.max)
 
         gate = tile("gate", [P, PACK, O], F32)
         for t in range(PACK):
             bank = psum.tile([P, J], F32, name=f"bank{t}")
             nc.tensor.matmul_mx(out=bank[:], lhsT=w_dw[:, t * P : (t + 1) * P].bitcast(E4M3),
-                                lhsT_scale=planes_a[:, J + t * P : J + (t + 1) * P],
-                                rhs=xt_gw[:].bitcast(E2M1), rhs_scale=planes_a[:, :J], start=True, stop=True)
+                                lhsT_scale=planes_a[:, t * P : (t + 1) * P],
+                                rhs=xt_gw[:].bitcast(E2M1), rhs_scale=planes_a[:, R : R + J], start=True, stop=True)
             a_t = tile(f"a_rows{t}", [P, J], F32)
-            if t < 2:
-                nc.scalar.copy(a_t[:], bank[:])
-            else:
-                nc.vector.tensor_copy(a_t[:], bank[:])
+            empty(a_t[:], bank[:], t in ())
             nc.scalar.activation(out=gate[:, t, :], in_=a_t[:].indirect(idx4[:]), func=ACT.Sigmoid, scale=slope[:, t : t + 1])
-
-        xo_gw = gather("xo_gw", xo_w, idx2, J, U32)
-        w2_dw = tile("w2_dw", [P, R], U16)
-        deal(w2_dw[:], w2_w[:], 8)
-
-        b3 = tile("b3", [P, PACK, O], F32)
-        b4 = tile("b4", [P, PACK, O], F32)
-        top = tile("top", [P, PACK, O], F32)
-        for half in range(2):
-            bank = psum.tile([P, 2 * J], F32, name=f"bank{PACK + half}")
-            for u in range(2):
-                t = 2 * half + u
-                nc.tensor.matmul_mx(out=bank[:, u * J : (u + 1) * J], lhsT=w2_dw[:, t * P : (t + 1) * P].bitcast(E2M1),
-                                    lhsT_scale=planes_b[:, J + t * P : J + (t + 1) * P],
-                                    rhs=xo_gw[:].bitcast(E4M3), rhs_scale=planes_b[:, :J], start=True, stop=True)
-            b_pair = tile(f"b_pair{half}", [P, 2 * J], F32)
-            if half == 0:
-                nc.vector.tensor_copy(b_pair[:], bank[:])
-            else:
-                nc.scalar.copy(b_pair[:], bank[:])
-            for u in range(2):
-                t = 2 * half + u
-                b_t = b_pair[:, u * J : (u + 1) * J]
-                if t < 1:
-                    nc.vector.tensor_copy(b3[:, t, :], b_t.indirect(idx3[:]))
-                else:
-                    nc.scalar.activation(out=b3[:, t, :], in_=b_t.indirect(idx3[:]), func=ACT.Copy)
-                if t < 3:
-                    nc.vector.tensor_copy(b4[:, t, :], b_t.indirect(idx4[:]))
-                else:
-                    nc.scalar.activation(out=b4[:, t, :], in_=b_t.indirect(idx4[:]), func=ACT.Copy)
-                nc.vector.tensor_tensor(top[:, t, :], b3[:, t, :], b4[:, t, :], ALU.max)
 
         hid = tile("hid", [P, O, PACK], BF16)
         nc.vector.tensor_tensor(
@@ -166,8 +155,8 @@ def tile_list_twotab_agree_one_scattered_kernel(tc, xt_words, xt_scales, w_words
 
         for h in range(2):
             rows = slice(h * P, (h + 1) * P)
-            bank = psum.tile([P, O], F32, name=f"bank{h}")
-            nc.tensor.matmul_mx(out=bank[:], lhsT=wb_w[:, rows].bitcast(E2M1), lhsT_scale=planes_b[:, J + R + h * P : J + R + (h + 1) * P],
+            bank = psum.tile([P, O], F32, name=f"bank{PACK + h}")
+            nc.tensor.matmul_mx(out=bank[:], lhsT=wb_w[:, rows].bitcast(E2M1), lhsT_scale=planes_a[:, J + R + h * P : J + R + (h + 1) * P],
                                 rhs=hid_w[:].bitcast(E5M2), rhs_scale=hid_s[:], start=True, stop=True)
             p_h = tile(f"p{h}", [P, O], F32)
             if h == 0:

@@ -67,8 +67,8 @@ def tile_list_twotab_agree_one_scattered_kernel(tc, xt_words, xt_scales, w_words
         nc.gpsimd.memset(warm[:, 0:1], 0.0)
         nc.scalar.activation(out=warm[:, 1:2], in_=warm[:, 0:1], func=ACT.Sigmoid)
 
-        xo_s = zeroed_plane("xo_s", Z)
         w_s = zeroed_plane("w_s", R)
+        xo_s = zeroed_plane("xo_s", Z)
         xt_s = zeroed_plane("xt_s", T)
         stage = tile("stage", [P, J + R + J + N], U8)
         planes_a = zeroed_plane("planes_a", R + J + N)
@@ -78,29 +78,29 @@ def tile_list_twotab_agree_one_scattered_kernel(tc, xt_words, xt_scales, w_words
 
         idx2 = load_list("idx2", offs2)
         idx = load_list("idx", offs)
-        load_scale_rows(xo_s[:], 0, xo_scales, nc.sync)
         load_scale_rows(w_s[:], 0, w2_scales, nc.sync)
         load_scale_rows(w_s[:], 16, w_scales, nc.sync)
+        load_scale_rows(xo_s[:], 0, xo_scales, nc.sync)
         load_scale_rows(xt_s[:], 16, xt_scales, nc.sync)
+        load_scale_rows(stage[:, J + R + J :], 16, wb_scales, nc.sync)
         xo_w = load_words("xo_w", xo_words[0].rearrange("p n t -> p (n t)"), Z, U32, nc.sync)
         w2_w = load_words("w2_w", w2_words[0], R, U16, nc.sync)
-        xt_w = load_words("xt_w", xt_words[0], T, U16, nc.sync)
         idx4 = load_list("idx4", offs4)
         idx3 = load_list("idx3", offs3)
-        idx5 = load_list("idx5", offs5)
-        w_w = load_words("w_w", w_words[0].rearrange("p n t -> p (n t)"), R, U32, nc.sync)
-        load_scale_rows(stage[:, J + R + J :], 16, wb_scales, nc.gpsimd)
+        xt_w = load_words("xt_w", xt_words[0], T, U16, nc.sync)
         slope = tile("slope", [P, PACK], F32)
         nc.gpsimd.dma_start(slope[:], sg.rearrange("(p t) o -> p (t o)", t=PACK))
         wb_w = load_words("wb_w", wb_words[0], N, U16, nc.gpsimd)
 
-        xo_gs = gather("xo_gs", xo_s, idx2, J, U8)
         deal(stage[:, J : J + R], w_s[:], 16)
+        xo_gs = gather("xo_gs", xo_s, idx2, J, U8)
         nc.vector.tensor_copy(stage[:, :J].bitcast(I32), xo_gs[:].bitcast(I32))
         spread_scale_rows(stage[:, : J + R], stage[:, : J + R], 0, range(1, 4))
+        w_w = load_words("w_w", w_words[0].rearrange("p n t -> p (n t)"), R, U32, nc.sync)
         xt_gs = gather("xt_gs", xt_s, idx, J, U8)
         nc.vector.tensor_copy(stage[:, J + R : J + R + J].bitcast(I32), xt_gs[:].bitcast(I32))
         spread_scale_rows(planes_a[:], stage[:, J:], 16, range(4))
+        idx5 = load_list("idx5", offs5)
         xo_gw = gather("xo_gw", xo_w, idx2, J, U32)
         w2_dw = tile("w2_dw", [P, R], U16)
         deal(w2_dw[:], w2_w[:], 8)
@@ -145,13 +145,17 @@ def tile_list_twotab_agree_one_scattered_kernel(tc, xt_words, xt_scales, w_words
             nc.scalar.activation(out=gate[:, t, :], in_=a_t[:].indirect(idx4[:]), func=ACT.Sigmoid, scale=slope[:, t : t + 1])
 
         hid = tile("hid", [P, O, PACK], BF16)
-        nc.vector.tensor_tensor(
-            hid[:].rearrange("p (c i) t -> p c t i", i=4),
-            top[:].rearrange("p t (c i) -> p c t i", i=4),
-            gate[:].rearrange("p t (c i) -> p c t i", i=4), ALU.mult)
         hid_w = tile("hid_w", [P, O], U32)
         hid_s = tile("hid_s", [P, O], U8)
-        nc.vector.quantize_mx(out=hid_w[:].bitcast(E5M2), scales=hid_s[:], in_=hid[:].rearrange("p o t -> p (o t)"))
+        halves = [slice(0, O // 2), slice(O // 2, O)]
+        for places in halves:
+            nc.vector.tensor_tensor(
+                hid[:, places, :].rearrange("p (c i) t -> p c t i", i=4),
+                top[:, :, places].rearrange("p t (c i) -> p c t i", i=4),
+                gate[:, :, places].rearrange("p t (c i) -> p c t i", i=4), ALU.mult)
+        for places in halves:
+            nc.vector.quantize_mx(out=hid_w[:, places].bitcast(E5M2), scales=hid_s[:, places],
+                                  in_=hid[:, places, :].rearrange("p o t -> p (o t)"))
 
         for h in range(2):
             rows = slice(h * P, (h + 1) * P)

from contextlib import ExitStack

import concourse.mybir as mybir

F32 = mybir.dt.float32
BF16 = mybir.dt.bfloat16
I32 = mybir.dt.int32
U32 = mybir.dt.uint32
U16 = mybir.dt.uint16
U8 = mybir.dt.uint8
E4M3 = mybir.dt.float8_e4m3fn_x4
E5M2 = mybir.dt.float8_e5m2_x4
E2M1 = mybir.dt.float4_e2m1fn_x4
ACT = mybir.ActivationFunctionType
ALU = mybir.AluOpType

P = 128
PACK = 4
T, Z, J, R, O, N, E = 1024, 1024, 256, 512, 128, 256, 1024
FLOPS = 2 * 512 * R * J * 2 + 2 * R * N * O


def tile_list_twotab_agree_one_scattered_kernel(tc, xt_words, xt_scales, w_words, w_scales, xo_words, xo_scales,
        w2_words, w2_scales, sg, wb_words, wb_scales, offs, offs2, offs3, offs4, offs5, out):
    nc = tc.nc
    with ExitStack() as ctx:
        keep = ctx.enter_context(tc.tile_pool(name="keep", bufs=1))
        psum = ctx.enter_context(tc.psum_pool(name="psum", bufs=1))

        def tile(name, shape, dtype):
            return keep.tile(shape, dtype, name=name, align_bytes=64)

        def load_list(name, src):
            dst = keep.tile(list(src.shape), U16, name=name)
            nc.sync.dma_start(dst[:], src)
            return dst

        def load_words(name, src, columns, dtype, engine):
            dst = tile(name, [P, columns], dtype)
            engine.dma_start(dst[:].bitcast(I32), src.bitcast(I32))
            return dst

        def zeroed_plane(name, columns):
            plane = tile(name, [P, columns], U8)
            nc.vector.memset(plane[:].bitcast(I32), 0)
            return plane

        def load_scale_rows(dst, first, src, engine):
            engine.dma_start(dst.bitcast(I32)[first : first + 16, :], src[0].bitcast(I32))

        def spread_scale_rows(dst, src, first, quadrants):
            for q in quadrants:
                nc.sync.dma_start(dst.bitcast(I32)[32 * q : 32 * q + 4, :],
                                  src.bitcast(I32)[first + 4 * q : first + 4 * q + 4, :])

        def deal(dst, src, run):
            nc.vector.tensor_copy(
                out=dst.rearrange("p (t c i) -> p c t i", t=PACK, i=run),
                in_=src.rearrange("p (c i t) -> p c t i", i=run, t=PACK))

        def gather(name, window, offsets, columns, dtype):
            dst = tile(name, [P, columns], dtype)
            nc.vector.tensor_copy(dst[:], window[:].indirect(offsets[:]))
            return dst

        warm = tile("warm", [P, 2], F32)
        nc.gpsimd.memset(warm[:, 0:1], 0.0)
        nc.scalar.activation(out=warm[:, 1:2], in_=warm[:, 0:1], func=ACT.Sigmoid)

        w_s = zeroed_plane("w_s", R)
        xo_s = zeroed_plane("xo_s", Z)
        xt_s = zeroed_plane("xt_s", T)
        stage = tile("stage", [P, J + R + J + N], U8)
        planes_a = zeroed_plane("planes_a", R + J + N)
        pages = [tile(f"page{h}", [P, E], F32) for h in range(2)]
        for page in pages:
            nc.vector.memset(page[:], 0.0)

        idx2 = load_list("idx2", offs2)
        idx = load_list("idx", offs)
        load_scale_rows(w_s[:], 0, w2_scales, nc.sync)
        load_scale_rows(w_s[:], 16, w_scales, nc.sync)
        load_scale_rows(xo_s[:], 0, xo_scales, nc.sync)
        load_scale_rows(xt_s[:], 16, xt_scales, nc.sync)
        load_scale_rows(stage[:, J + R + J :], 16, wb_scales, nc.sync)
        xo_w = load_words("xo_w", xo_words[0].rearrange("p n t -> p (n t)"), Z, U32, nc.sync)
        w2_w = load_words("w2_w", w2_words[0], R, U16, nc.sync)
        idx4 = load_list("idx4", offs4)
        idx3 = load_list("idx3", offs3)
        xt_w = load_words("xt_w", xt_words[0], T, U16, nc.sync)
        slope = tile("slope", [P, PACK], F32)
        nc.gpsimd.dma_start(slope[:], sg.rearrange("(p t) o -> p (t o)", t=PACK))
        wb_w = load_words("wb_w", wb_words[0], N, U16, nc.gpsimd)

        deal(stage[:, J : J + R], w_s[:], 16)
        xo_gs = gather("xo_gs", xo_s, idx2, J, U8)
        nc.vector.tensor_copy(stage[:, :J].bitcast(I32), xo_gs[:].bitcast(I32))
        spread_scale_rows(stage[:, : J + R], stage[:, : J + R], 0, range(1, 4))
        w_w = load_words("w_w", w_words[0].rearrange("p n t -> p (n t)"), R, U32, nc.sync)
        xt_gs = gather("xt_gs", xt_s, idx, J, U8)
        nc.vector.tensor_copy(stage[:, J + R : J + R + J].bitcast(I32), xt_gs[:].bitcast(I32))
        spread_scale_rows(planes_a[:], stage[:, J:], 16, range(4))
        idx5 = load_list("idx5", offs5)
        xo_gw = gather("xo_gw", xo_w, idx2, J, U32)
        w2_dw = tile("w2_dw", [P, R], U16)
        deal(w2_dw[:], w2_w[:], 8)
        xt_gw = gather("xt_gw", xt_w, idx, J, U16)
        w_dw = tile("w_dw", [P, R], U32)
        deal(w_dw[:].bitcast(I32), w_w[:].bitcast(I32), 4)

        def empty(dst, bank, on_vector):
            if on_vector:
                nc.vector.tensor_copy(dst, bank)
            else:
                nc.scalar.copy(dst, bank)

        def pick(dst, window, offsets, on_vector):
            if on_vector:
                nc.vector.tensor_copy(dst, window[:].indirect(offsets[:]))
            else:
                nc.scalar.activation(out=dst, in_=window[:].indirect(offsets[:]), func=ACT.Copy)

        b3 = tile("b3", [P, PACK, O], F32)
        b4 = tile("b4", [P, PACK, O], F32)
        top = tile("top", [P, PACK, O], F32)
        for t in range(PACK):
            bank = psum.tile([P, J], F32, name=f"bank{PACK + t}")
            nc.tensor.matmul_mx(out=bank[:], lhsT=w2_dw[:, t * P : (t + 1) * P].bitcast(E2M1),
                                lhsT_scale=stage[:, J + t * P : J + (t + 1) * P],
                                rhs=xo_gw[:].bitcast(E4M3), rhs_scale=stage[:, :J], start=True, stop=True)
            b_t = tile(f"b_rows{t}", [P, J], F32)
            empty(b_t[:], bank[:], t in ())
            pick(b4[:, t, :], b_t, idx4, t in (0, 1, 2, 3,))
            pick(b3[:, t, :], b_t, idx3, t in (0, 1, 2, 3,))
        nc.vector.tensor_tensor(top[:], b3[:], b4[:], ALU.max)

        gate = tile("gate", [P, PACK, O], F32)
        for t in range(PACK):
            bank = psum.tile([P, J], F32, name=f"bank{t}")
            nc.tensor.matmul_mx(out=bank[:], lhsT=w_dw[:, t * P : (t + 1) * P].bitcast(E4M3),
                                lhsT_scale=planes_a[:, t * P : (t + 1) * P],
                                rhs=xt_gw[:].bitcast(E2M1), rhs_scale=planes_a[:, R : R + J], start=True, stop=True)
            a_t = tile(f"a_rows{t}", [P, J], F32)
            empty(a_t[:], bank[:], t in ())
            nc.scalar.activation(out=gate[:, t, :], in_=a_t[:].indirect(idx4[:]), func=ACT.Sigmoid, scale=slope[:, t : t + 1])

        hid = tile("hid", [P, O, PACK], BF16)
        hid_w = tile("hid_w", [P, O], U32)
        hid_s = tile("hid_s", [P, O], U8)
        halves = [slice(0, O // 2), slice(O // 2, O)]
        for places in halves:
            nc.vector.tensor_tensor(
                hid[:, places, :].rearrange("p (c i) t -> p c t i", i=4),
                top[:, :, places].rearrange("p t (c i) -> p c t i", i=4),
                gate[:, :, places].rearrange("p t (c i) -> p c t i", i=4), ALU.mult)
        for places in halves:
            nc.vector.quantize_mx(out=hid_w[:, places].bitcast(E5M2), scales=hid_s[:, places],
                                  in_=hid[:, places, :].rearrange("p o t -> p (o t)"))

        for h in range(2):
            rows = slice(h * P, (h + 1) * P)
            bank = psum.tile([P, O], F32, name=f"bank{PACK + h}")
            nc.tensor.matmul_mx(out=bank[:], lhsT=wb_w[:, rows].bitcast(E2M1), lhsT_scale=planes_a[:, J + R + h * P : J + R + (h + 1) * P],
                                rhs=hid_w[:].bitcast(E5M2), rhs_scale=hid_s[:], start=True, stop=True)
            p_h = tile(f"p{h}", [P, O], F32)
            if h == 0:
                nc.vector.tensor_copy(p_h[:], bank[:])
                nc.vector.tensor_copy(pages[h][:].indirect(idx5[:]), p_h[:])
                nc.sync.dma_start(out[rows, :], pages[h][:])
            else:
                nc.scalar.copy(p_h[:], bank[:])
                nc.scalar.activation(out=pages[h][:].indirect(idx5[:]), in_=p_h[:], func=ACT.Copy)
                nc.scalar.dma_start(out[rows, :], pages[h][:])
